import numpy as np
import ml_dtypes


def mxq(x, axis, fmt="e4m3"):
    dtype, down = {"e4m3": (ml_dtypes.float8_e4m3fn, 7), "e5m2": (ml_dtypes.float8_e5m2, 14)}[fmt]
    v = np.moveaxis(np.asarray(x, np.float32).astype(ml_dtypes.bfloat16).astype(np.float64), axis, -1)
    blocks = v.reshape(v.shape[:-1] + (-1, 32))
    amax = np.abs(blocks).max(-1, keepdims=True)
    byte = np.maximum(np.where(amax > 0, np.frexp(amax)[1] - 1 + 127, 0) - down, 1)
    scale = np.exp2(byte - 127.0)
    codes = (blocks / scale).astype(np.float32).astype(dtype).astype(np.float64)
    return np.moveaxis((codes * scale).reshape(v.shape), -1, axis)


WIDE = False


def mx_kscale(k, group=512):
    if not WIDE:
        return np.ones(k)
    levels = np.array([18, -18])
    if group != 512:
        return np.exp2(np.random.permutation(np.resize(levels, k // group))).repeat(group)
    if k % 512:
        return np.exp2(np.random.permutation(np.resize(levels, k // 32))).repeat(32)
    a = np.empty((k // 512, 16))
    for p in range(k // 512):
        a[p, :8] = np.random.permutation(np.resize(levels, 8))
        for g in range(8):
            far = levels[np.abs(levels - a[p, g]) >= 10]
            a[p, g + 8] = far[np.random.randint(len(far))]
    return np.exp2(a.ravel()).repeat(32)


def f64(x):
    return np.asarray(x).astype(np.float64)


def softplus(v):
    return np.log(1.0 + np.exp(v))


def sigmoid(v):
    return 1.0 / (1.0 + np.exp(-v))


G, D, M, O, N = 4, 128, 128, 128, 512


def setup_inputs():
    n = np.random.standard_normal
    s_d = mx_kscale(D, 0)
    s_o = mx_kscale(O, 0)
    return {
        "x": (n((G, D, N)) * s_d[:, None]).astype(np.float32),
        "w1": (n((G, D, M)) / np.sqrt(D) / s_d[:, None]).astype(np.float32),
        "w2": (n((G, D, M)) / np.sqrt(D) / s_d[:, None]).astype(np.float32),
        "re": (np.random.uniform(50.0, 200.0, (G, M, 1))).astype(np.float32),
        "wo": (n((G, O, M)) / np.sqrt(O) / s_o[:, None]).astype(np.float32),
        "dy": (n((G, O, N)) * s_o[:, None]).astype(np.float32),
        "old": (0.3 * n((G, M, N))).astype(np.float32),
    }


def reference(x, w1, w2, re, wo, dy, old):
    w1q = mxq(f64(w1), 1, "e4m3")
    xq = mxq(f64(x), 1, "e4m3")
    z1 = w1q.transpose(0, 2, 1) @ xq
    w2q = mxq(f64(w2), 1, "e4m3")
    z2 = w2q.transpose(0, 2, 1) @ xq
    p1 = softplus(z1)
    zs = np.sum(p1, axis=-1, keepdims=True) + f64(re)
    woq = mxq(f64(wo), 1, "e4m3")
    dyq = mxq(f64(dy), 1, "e4m3")
    c0 = woq.transpose(0, 2, 1) @ dyq
    dzs = np.sum(c0 * 512.0 * np.tanh(z2) * p1 / np.square(zs) * (-1.0), axis=-1, keepdims=True)
    dp1 = c0 * 512.0 * np.tanh(z2) / zs + dzs
    dz1 = dp1 * sigmoid(z1)
    y = dz1 + f64(old)
    return y

@@ -1,0 +1,180 @@
+from contextlib import ExitStack
+
+import concourse.mybir as mybir
+
+G, D, M, N = 4, 128, 128, 512
+P = 128
+PACK = 4
+ROWS = D // PACK
+HALF = N // 2
+RUN = 4
+TINY = 2.0 ** -63
+
+F32 = mybir.dt.float32
+BF16 = mybir.dt.bfloat16
+U32 = mybir.dt.uint32
+U8 = mybir.dt.uint8
+FP8X4 = mybir.dt.float8_e4m3fn_x4
+ACT = mybir.ActivationFunctionType
+ALU = mybir.AluOpType
+
+FLOPS = 3 * 2 * G * D * M * N
+
+
+def tile_rows_browshare_kernel(tc, x, w1, w2, re, wo, dy, old, out):
+    nc = tc.nc
+    with ExitStack() as ctx:
+        sb = ctx.enter_context(tc.tile_pool(name="sb", bufs=1))
+        ps = ctx.enter_context(tc.psum_pool(name="ps", bufs=1))
+        ctx.enter_context(tc.manual_schedule())
+
+        def load(name, src, c0, width):
+            raw = sb.tile([P, PACK, width], F32, name=name + "_raw", align_bytes=64)
+            rows = src.rearrange("g (p j) c -> (g p) j c", j=PACK)
+            nc.sync.dma_start(out=raw[:], in_=rows[:, :, c0 : c0 + width])
+            return raw
+
+        def interleave(dst, raw):
+            nc.vector.tensor_copy(
+                out=dst.rearrange("p (c i j) -> p c j i", i=RUN, j=PACK),
+                in_=raw[:].rearrange("p j (c i) -> p c j i", i=RUN),
+            )
+
+        def quantize(codes, scales, src):
+            nc.vector.quantize_mx(out=codes.bitcast(FP8X4), scales=scales, in_=src)
+
+        def operand(name, width):
+            codes = sb.tile([P, width], U32, name=name + "_codes", align_bytes=64)
+            scales = sb.tile([P, width], U8, name=name + "_scales", align_bytes=64)
+            return codes, scales
+
+        def bf16_tile(name, width):
+            grouped = sb.tile([P, PACK * width], BF16, name=name + "_bf16", align_bytes=64)
+            return grouped
+
+        def product(bank, g, w, c0, a):
+            rows = slice(ROWS * g, ROWS * (g + 1))
+            nc.tensor.matmul_mx(
+                out=bank[:],
+                lhsT=w[0][rows, c0 : c0 + M].bitcast(FP8X4),
+                lhsT_scale=w[1][rows, c0 : c0 + M],
+                rhs=a[0][rows, :].bitcast(FP8X4),
+                rhs_scale=a[1][rows, :],
+                start=True,
+                stop=True,
+            )
+
+        def per_group(name):
+            return [sb.tile([P, N], F32, name=name + str(g), align_bytes=64) for g in range(G)]
+
+        w1_raw = load("w1", w1, 0, M)
+        x_raw = [load("x" + str(h), x, h * HALF, HALF) for h in range(2)]
+        w2_raw = load("w2", w2, 0, M)
+        wo_raw = load("wo", wo, 0, M)
+        dy_raw = [load("dy" + str(h), dy, h * HALF, HALF) for h in range(2)]
+        reserve = sb.tile([P, G], F32, name="reserve")
+        with nc.allow_non_contiguous_dma(reason="one reserve for each partition and group"):
+            nc.sync.dma_start(out=reserve[:], in_=re.rearrange("g m o -> m (g o)"))
+        old_sb = sb.tile([P, G, N], F32, name="old_sb")
+        nc.sync.dma_start(out=old_sb[:], in_=old.rearrange("g m n -> m g n"))
+
+        tiny = sb.tile([P, 1], F32, name="tiny")
+        nc.vector.memset(tiny[:], TINY)
+
+        w1_q, w2o_q, x_q, dy_q = operand("w1", M), operand("w2o", 2 * M), operand("x", N), operand("dy", N)
+        w1_b, w2o_b = bf16_tile("w1", M), bf16_tile("w2o", 2 * M)
+        x_b = [bf16_tile("x" + str(h), HALF) for h in range(2)]
+        dy_b = [bf16_tile("dy" + str(h), HALF) for h in range(2)]
+
+        def half(q, h):
+            return q[0][:, h * HALF : (h + 1) * HALF], q[1][:, h * HALF : (h + 1) * HALF]
+
+        z1_bank = [ps.tile([P, N], F32, name="z1_bank" + str(g)) for g in range(G)]
+        z2_bank = [ps.tile([P, N], F32, name="z2_bank" + str(g)) for g in range(G)]
+        q, t, lnq, p1, a, s, u, res = [per_group(n) for n in ("q", "t", "lnq", "p1", "a", "s", "u", "res")]
+        sums = sb.tile([P, G], F32, name="sums")
+        nzs = sb.tile([P, G], F32, name="nzs")
+        nrz = sb.tile([P, G], F32, name="nrz")
+        shift = sb.tile([P, G], F32, name="shift")
+
+        interleave(w1_b[:], w1_raw)
+        quantize(w1_q[0][:], w1_q[1][:], w1_b[:])
+        for h in range(2):
+            interleave(x_b[h][:], x_raw[h])
+            quantize(*half(x_q, h), x_b[h][:])
+        for g in range(G):
+            product(z1_bank[g], g, w1_q, 0, x_q)
+        for g in range(G):
+            nc.scalar.activation(out=q[g][:], in_=z1_bank[g][:], func=ACT.Sigmoid, scale=-1.0)
+
+        interleave(w2o_b[:, : PACK * M], w2_raw)
+        interleave(w2o_b[:, PACK * M :], wo_raw)
+        quantize(w2o_q[0][:], w2o_q[1][:], w2o_b[:])
+        for g in range(G):
+            product(z2_bank[g], g, w2o_q, 0, x_q)
+        for g in range(G):
+            nc.scalar.activation(out=t[g][:], in_=z2_bank[g][:], func=ACT.Tanh)
+
+        for h in range(2):
+            interleave(dy_b[h][:], dy_raw[h])
+            quantize(*half(dy_q, h), dy_b[h][:])
+        for g in range(G):
+            product(z2_bank[g], g, w2o_q, M, dy_q)
+        for g in range(G):
+            nc.vector.tensor_tensor(out=a[g][:], in0=z2_bank[g][:], in1=t[g][:], op=ALU.mult)
+
+        for g in range(G):
+            nc.scalar.activation(out=lnq[g][:], in_=q[g][:], func=ACT.Ln, bias=tiny[:])
+        for g in range(G):
+            nc.scalar.activation(out=s[g][:], in_=q[g][:], func=ACT.Copy, scale=512.0, bias=-512.0)
+
+        def softplus(g):
+            nc.vector.scalar_tensor_tensor(
+                out=p1[g][:], in0=lnq[g][:], scalar=-1.0, in1=z1_bank[g][:],
+                op0=ALU.mult, op1=ALU.max, accum_out=sums[:, g : g + 1])
+
+        def neg_total(gs):
+            nc.vector.scalar_tensor_tensor(
+                out=nzs[:, gs], in0=sums[:, gs], scalar=-1.0, in1=reserve[:, gs],
+                op0=ALU.mult, op1=ALU.subtract)
+
+        def invert(gs):
+            nc.vector.reciprocal(out=nrz[:, gs], in_=nzs[:, gs])
+
+        def row_shift(g):
+            nc.vector.scalar_tensor_tensor(
+                out=lnq[g][:], in0=a[g][:], scalar=nrz[:, g : g + 1], in1=p1[g][:],
+                op0=ALU.mult, op1=ALU.mult, accum_out=shift[:, g : g + 1])
+
+        def gate(g):
+            nc.vector.scalar_tensor_tensor(
+                out=u[g][:], in0=a[g][:], scalar=shift[:, g : g + 1], in1=s[g][:],
+                op0=ALU.add, op1=ALU.mult)
+
+        def finish(g):
+            nc.vector.scalar_tensor_tensor(
+                out=res[g][:], in0=u[g][:], scalar=nrz[:, g : g + 1], in1=old_sb[:, g, :],
+                op0=ALU.mult, op1=ALU.add)
+            nc.sync.dma_start(out=out[g], in_=res[g][:])
+
+        first, second = slice(0, 2), slice(2, 4)
+        softplus(0)
+        softplus(1)
+        softplus(2)
+        neg_total(first)
+        softplus(3)
+        invert(first)
+        neg_total(second)
+        row_shift(0)
+        invert(second)
+        row_shift(1)
+        gate(0)
+        row_shift(2)
+        finish(0)
+        gate(1)
+        row_shift(3)
+        finish(1)
+        gate(2)
+        gate(3)
+        finish(2)
+        finish(3)

@@ -8,6 +8,7 @@ PACK = 4
 ROWS = D // PACK
 HALF = N // 2
 RUN = 4
+STEP = 128
 TINY = 2.0 ** -63
 
 F32 = mybir.dt.float32
@@ -52,24 +53,27 @@ def tile_rows_browshare_kernel(tc, x, w1, w2, re, wo, dy, old, out):
             grouped = sb.tile([P, PACK * width], BF16, name=name + "_bf16", align_bytes=64)
             return grouped
 
-        def product(bank, g, w, c0, a):
+        def product(bank, g, w, a, n0, n1):
             rows = slice(ROWS * g, ROWS * (g + 1))
-            nc.tensor.matmul_mx(
-                out=bank[:],
-                lhsT=w[0][rows, c0 : c0 + M].bitcast(FP8X4),
-                lhsT_scale=w[1][rows, c0 : c0 + M],
-                rhs=a[0][rows, :].bitcast(FP8X4),
-                rhs_scale=a[1][rows, :],
-                start=True,
-                stop=True,
-            )
+            for c in range(n0, n1, STEP):
+                cols = slice(c, c + STEP)
+                nc.tensor.matmul_mx(
+                    out=bank[:, cols],
+                    lhsT=w[0][rows, :].bitcast(FP8X4),
+                    lhsT_scale=w[1][rows, :],
+                    rhs=a[0][rows, cols].bitcast(FP8X4),
+                    rhs_scale=a[1][rows, cols],
+                    start=True,
+                    stop=True,
+                )
 
         def per_group(name):
             return [sb.tile([P, N], F32, name=name + str(g), align_bytes=64) for g in range(G)]
 
+        x_raw = [load("x0", x, 0, HALF)]
         w1_raw = load("w1", w1, 0, M)
-        x_raw = [load("x" + str(h), x, h * HALF, HALF) for h in range(2)]
         w2_raw = load("w2", w2, 0, M)
+        x_raw.append(load("x1", x, HALF, HALF))
         wo_raw = load("wo", wo, 0, M)
         dy_raw = [load("dy" + str(h), dy, h * HALF, HALF) for h in range(2)]
         reserve = sb.tile([P, G], F32, name="reserve")
@@ -81,8 +85,9 @@ def tile_rows_browshare_kernel(tc, x, w1, w2, re, wo, dy, old, out):
         tiny = sb.tile([P, 1], F32, name="tiny")
         nc.vector.memset(tiny[:], TINY)
 
-        w1_q, w2o_q, x_q, dy_q = operand("w1", M), operand("w2o", 2 * M), operand("x", N), operand("dy", N)
-        w1_b, w2o_b = bf16_tile("w1", M), bf16_tile("w2o", 2 * M)
+        w1_q, w2_q, wo_q = operand("w1", M), operand("w2", M), operand("wo", M)
+        x_q, dy_q = operand("x", N), operand("dy", N)
+        w1_b, w2_b, wo_b = bf16_tile("w1", M), bf16_tile("w2", M), bf16_tile("wo", M)
         x_b = [bf16_tile("x" + str(h), HALF) for h in range(2)]
         dy_b = [bf16_tile("dy" + str(h), HALF) for h in range(2)]
 
@@ -97,46 +102,53 @@ def tile_rows_browshare_kernel(tc, x, w1, w2, re, wo, dy, old, out):
         nrz = sb.tile([P, G], F32, name="nrz")
         shift = sb.tile([P, G], F32, name="shift")
 
-        interleave(w1_b[:], w1_raw)
-        quantize(w1_q[0][:], w1_q[1][:], w1_b[:])
-        for h in range(2):
-            interleave(x_b[h][:], x_raw[h])
-            quantize(*half(x_q, h), x_b[h][:])
-        for g in range(G):
-            product(z1_bank[g], g, w1_q, 0, x_q)
-        for g in range(G):
-            nc.scalar.activation(out=q[g][:], in_=z1_bank[g][:], func=ACT.Sigmoid, scale=-1.0)
+        def forward(h):
+            cols = slice(h * HALF, (h + 1) * HALF)
+            for g in range(G):
+                product(z1_bank[g], g, w1_q, x_q, cols.start, cols.stop)
+            for g in range(G):
+                product(z2_bank[g], g, w2_q, x_q, cols.start, cols.stop)
+            for g in range(G):
+                nc.scalar.activation(out=q[g][:, cols], in_=z1_bank[g][:, cols], func=ACT.Sigmoid, scale=-1.0)
+            for g in range(G):
+                nc.scalar.activation(out=t[g][:, cols], in_=z2_bank[g][:, cols], func=ACT.Tanh)
 
-        interleave(w2o_b[:, : PACK * M], w2_raw)
-        interleave(w2o_b[:, PACK * M :], wo_raw)
-        quantize(w2o_q[0][:], w2o_q[1][:], w2o_b[:])
-        for g in range(G):
-            product(z2_bank[g], g, w2o_q, 0, x_q)
-        for g in range(G):
-            nc.scalar.activation(out=t[g][:], in_=z2_bank[g][:], func=ACT.Tanh)
+        interleave(x_b[0][:], x_raw[0])
+        interleave(w1_b[:], w1_raw)
+        quantize(*half(x_q, 0), x_b[0][:])
+        quantize(w1_q[0][:], w1_q[1][:], w1_b[:])
+        interleave(w2_b[:], w2_raw)
+        quantize(w2_q[0][:], w2_q[1][:], w2_b[:])
+        forward(0)
+        interleave(x_b[1][:], x_raw[1])
+        interleave(wo_b[:], wo_raw)
+        quantize(*half(x_q, 1), x_b[1][:])
+        quantize(wo_q[0][:], wo_q[1][:], wo_b[:])
+        forward(1)
 
         for h in range(2):
             interleave(dy_b[h][:], dy_raw[h])
             quantize(*half(dy_q, h), dy_b[h][:])
-        for g in range(G):
-            product(z2_bank[g], g, w2o_q, M, dy_q)
+            for g in range(2):
+                product(z2_bank[g], g, wo_q, dy_q, h * HALF, (h + 1) * HALF)
+        for g in range(2, G):
+            product(z2_bank[g], g, wo_q, dy_q, 0, N)
         for g in range(G):
             nc.vector.tensor_tensor(out=a[g][:], in0=z2_bank[g][:], in1=t[g][:], op=ALU.mult)
 
-        for g in range(G):
+        def log(g):
             nc.scalar.activation(out=lnq[g][:], in_=q[g][:], func=ACT.Ln, bias=tiny[:])
-        for g in range(G):
-            nc.scalar.activation(out=s[g][:], in_=q[g][:], func=ACT.Copy, scale=512.0, bias=-512.0)
+
+        def sigmoid(g):
+            nc.scalar.activation(out=s[g][:], in_=q[g][:], func=ACT.Copy, scale=-512.0, bias=512.0)
 
         def softplus(g):
             nc.vector.scalar_tensor_tensor(
                 out=p1[g][:], in0=lnq[g][:], scalar=-1.0, in1=z1_bank[g][:],
                 op0=ALU.mult, op1=ALU.max, accum_out=sums[:, g : g + 1])
 
-        def neg_total(gs):
-            nc.vector.scalar_tensor_tensor(
-                out=nzs[:, gs], in0=sums[:, gs], scalar=-1.0, in1=reserve[:, gs],
-                op0=ALU.mult, op1=ALU.subtract)
+        def total(g):
+            nc.scalar.activation(out=nzs[:, g : g + 1], in_=sums[:, g : g + 1], func=ACT.Identity, bias=reserve[:, g : g + 1])
 
         def invert(gs):
             nc.vector.reciprocal(out=nrz[:, gs], in_=nzs[:, gs])
@@ -149,24 +161,33 @@ def tile_rows_browshare_kernel(tc, x, w1, w2, re, wo, dy, old, out):
         def gate(g):
             nc.vector.scalar_tensor_tensor(
                 out=u[g][:], in0=a[g][:], scalar=shift[:, g : g + 1], in1=s[g][:],
-                op0=ALU.add, op1=ALU.mult)
+                op0=ALU.subtract, op1=ALU.mult)
 
-        def finish(g):
+        def finish(g, cols=slice(0, N), queue=nc.sync):
             nc.vector.scalar_tensor_tensor(
-                out=res[g][:], in0=u[g][:], scalar=nrz[:, g : g + 1], in1=old_sb[:, g, :],
+                out=res[g][:, cols], in0=u[g][:, cols], scalar=nrz[:, g : g + 1], in1=old_sb[:, g, cols],
                 op0=ALU.mult, op1=ALU.add)
-            nc.sync.dma_start(out=out[g], in_=res[g][:])
+            queue.dma_start(out=out[g, :, cols], in_=res[g][:, cols])
 
-        first, second = slice(0, 2), slice(2, 4)
+        log(0)
         softplus(0)
+        log(1)
         softplus(1)
+        log(2)
+        total(0)
         softplus(2)
-        neg_total(first)
+        log(3)
+        total(1)
+        invert(slice(0, 1))
         softplus(3)
-        invert(first)
-        neg_total(second)
+        sigmoid(0)
+        total(2)
+        total(3)
+        for g in range(1, G):
+            sigmoid(g)
+        invert(slice(1, 2))
         row_shift(0)
-        invert(second)
+        invert(slice(2, 4))
         row_shift(1)
         gate(0)
         row_shift(2)
@@ -177,4 +198,5 @@ def tile_rows_browshare_kernel(tc, x, w1, w2, re, wo, dy, old, out):
         gate(2)
         gate(3)
         finish(2)
-        finish(3)
+        finish(3, slice(0, HALF), nc.scalar)
+        finish(3, slice(HALF, N))

@@ -102,39 +102,54 @@ def tile_rows_browshare_kernel(tc, x, w1, w2, re, wo, dy, old, out):
         nrz = sb.tile([P, G], F32, name="nrz")
         shift = sb.tile([P, G], F32, name="shift")
 
-        def forward(h):
-            cols = slice(h * HALF, (h + 1) * HALF)
+        def columns(h):
+            return slice(h * HALF, (h + 1) * HALF)
+
+        def products(banks, w, moving, h):
             for g in range(G):
-                product(z1_bank[g], g, w1_q, x_q, cols.start, cols.stop)
+                product(banks[g], g, w, moving, h * HALF, (h + 1) * HALF)
+
+        def sigmoids(h):
             for g in range(G):
-                product(z2_bank[g], g, w2_q, x_q, cols.start, cols.stop)
+                nc.scalar.activation(out=q[g][:, columns(h)], in_=z1_bank[g][:, columns(h)], func=ACT.Sigmoid, scale=-1.0)
+
+        def tanhs(h):
             for g in range(G):
-                nc.scalar.activation(out=q[g][:, cols], in_=z1_bank[g][:, cols], func=ACT.Sigmoid, scale=-1.0)
-            for g in range(G):
-                nc.scalar.activation(out=t[g][:, cols], in_=z2_bank[g][:, cols], func=ACT.Tanh)
+                nc.scalar.activation(out=t[g][:, columns(h)], in_=z2_bank[g][:, columns(h)], func=ACT.Tanh)
+
+        def gradient(g, h):
+            nc.vector.tensor_tensor(out=a[g][:, columns(h)], in0=z2_bank[g][:, columns(h)], in1=t[g][:, columns(h)], op=ALU.mult)
 
         interleave(x_b[0][:], x_raw[0])
         interleave(w1_b[:], w1_raw)
         quantize(*half(x_q, 0), x_b[0][:])
         quantize(w1_q[0][:], w1_q[1][:], w1_b[:])
+        products(z1_bank, w1_q, x_q, 0)
+        sigmoids(0)
         interleave(w2_b[:], w2_raw)
         quantize(w2_q[0][:], w2_q[1][:], w2_b[:])
-        forward(0)
+        products(z2_bank, w2_q, x_q, 0)
+        tanhs(0)
         interleave(x_b[1][:], x_raw[1])
-        interleave(wo_b[:], wo_raw)
         quantize(*half(x_q, 1), x_b[1][:])
-        quantize(wo_q[0][:], wo_q[1][:], wo_b[:])
-        forward(1)
+        products(z2_bank, w2_q, x_q, 1)
+        tanhs(1)
+        products(z1_bank, w1_q, x_q, 1)
+        sigmoids(1)
 
-        for h in range(2):
-            interleave(dy_b[h][:], dy_raw[h])
-            quantize(*half(dy_q, h), dy_b[h][:])
-            for g in range(2):
-                product(z2_bank[g], g, wo_q, dy_q, h * HALF, (h + 1) * HALF)
-        for g in range(2, G):
-            product(z2_bank[g], g, wo_q, dy_q, 0, N)
+        interleave(wo_b[:], wo_raw)
+        quantize(wo_q[0][:], wo_q[1][:], wo_b[:])
+        interleave(dy_b[0][:], dy_raw[0])
+        quantize(*half(dy_q, 0), dy_b[0][:])
+        products(z2_bank, wo_q, dy_q, 0)
+        interleave(dy_b[1][:], dy_raw[1])
+        gradient(0, 0)
+        quantize(*half(dy_q, 1), dy_b[1][:])
+        for g in range(1, G):
+            gradient(g, 0)
+        products(z2_bank, wo_q, dy_q, 1)
         for g in range(G):
-            nc.vector.tensor_tensor(out=a[g][:], in0=z2_bank[g][:], in1=t[g][:], op=ALU.mult)
+            gradient(g, 1)
 
         def log(g):
             nc.scalar.activation(out=lnq[g][:], in_=q[g][:], func=ACT.Ln, bias=tiny[:])

@@ -9,6 +9,7 @@ ROWS = D // PACK
 HALF = N // 2
 RUN = 4
 STEP = 128
+SHARE = 512.0
 TINY = 2.0 ** -63
 
 F32 = mybir.dt.float32
@@ -29,22 +30,26 @@ def tile_rows_browshare_kernel(tc, x, w1, w2, re, wo, dy, old, out):
         ps = ctx.enter_context(tc.psum_pool(name="ps", bufs=1))
         ctx.enter_context(tc.manual_schedule())
 
-        def load(name, src, c0, width):
-            raw = sb.tile([P, PACK, width], F32, name=name + "_raw", align_bytes=64)
+        def columns(h):
+            return slice(h * HALF, (h + 1) * HALF)
+
+        def load(name, src, cols):
+            raw = sb.tile([P, PACK, cols.stop - cols.start], F32, name=name + "_raw", align_bytes=64)
             rows = src.rearrange("g (p j) c -> (g p) j c", j=PACK)
-            nc.sync.dma_start(out=raw[:], in_=rows[:, :, c0 : c0 + width])
+            nc.sync.dma_start(out=raw[:], in_=rows[:, :, cols])
             return raw
 
-        def interleave(dst, raw):
+        def interleave(grouped, raw):
             nc.vector.tensor_copy(
-                out=dst.rearrange("p (c i j) -> p c j i", i=RUN, j=PACK),
+                out=grouped[:].rearrange("p (c i j) -> p c j i", i=RUN, j=PACK),
                 in_=raw[:].rearrange("p j (c i) -> p c j i", i=RUN),
             )
 
-        def quantize(codes, scales, src):
-            nc.vector.quantize_mx(out=codes.bitcast(FP8X4), scales=scales, in_=src)
+        def quantize(operand, cols, grouped):
+            codes, scales = operand
+            nc.vector.quantize_mx(out=codes[:, cols].bitcast(FP8X4), scales=scales[:, cols], in_=grouped[:])
 
-        def operand(name, width):
+        def mx_operand(name, width):
             codes = sb.tile([P, width], U32, name=name + "_codes", align_bytes=64)
             scales = sb.tile([P, width], U8, name=name + "_scales", align_bytes=64)
             return codes, scales
@@ -53,29 +58,16 @@ def tile_rows_browshare_kernel(tc, x, w1, w2, re, wo, dy, old, out):
             grouped = sb.tile([P, PACK * width], BF16, name=name + "_bf16", align_bytes=64)
             return grouped
 
-        def product(bank, g, w, a, n0, n1):
-            rows = slice(ROWS * g, ROWS * (g + 1))
-            for c in range(n0, n1, STEP):
-                cols = slice(c, c + STEP)
-                nc.tensor.matmul_mx(
-                    out=bank[:, cols],
-                    lhsT=w[0][rows, :].bitcast(FP8X4),
-                    lhsT_scale=w[1][rows, :],
-                    rhs=a[0][rows, cols].bitcast(FP8X4),
-                    rhs_scale=a[1][rows, cols],
-                    start=True,
-                    stop=True,
-                )
-
         def per_group(name):
             return [sb.tile([P, N], F32, name=name + str(g), align_bytes=64) for g in range(G)]
 
-        x_raw = [load("x0", x, 0, HALF)]
-        w1_raw = load("w1", w1, 0, M)
-        w2_raw = load("w2", w2, 0, M)
-        x_raw.append(load("x1", x, HALF, HALF))
-        wo_raw = load("wo", wo, 0, M)
-        dy_raw = [load("dy" + str(h), dy, h * HALF, HALF) for h in range(2)]
+        all_m = slice(0, M)
+        x_raw = [load("x0", x, columns(0))]
+        w1_raw = load("w1", w1, all_m)
+        w2_raw = load("w2", w2, all_m)
+        x_raw.append(load("x1", x, columns(1)))
+        wo_raw = load("wo", wo, all_m)
+        dy_raw = [load("dy" + str(h), dy, columns(h)) for h in range(2)]
         reserve = sb.tile([P, G], F32, name="reserve")
         with nc.allow_non_contiguous_dma(reason="one reserve for each partition and group"):
             nc.sync.dma_start(out=reserve[:], in_=re.rearrange("g m o -> m (g o)"))
@@ -85,29 +77,34 @@ def tile_rows_browshare_kernel(tc, x, w1, w2, re, wo, dy, old, out):
         tiny = sb.tile([P, 1], F32, name="tiny")
         nc.vector.memset(tiny[:], TINY)
 
-        w1_q, w2_q, wo_q = operand("w1", M), operand("w2", M), operand("wo", M)
-        x_q, dy_q = operand("x", N), operand("dy", N)
-        w1_b, w2_b, wo_b = bf16_tile("w1", M), bf16_tile("w2", M), bf16_tile("wo", M)
-        x_b = [bf16_tile("x" + str(h), HALF) for h in range(2)]
-        dy_b = [bf16_tile("dy" + str(h), HALF) for h in range(2)]
-
-        def half(q, h):
-            return q[0][:, h * HALF : (h + 1) * HALF], q[1][:, h * HALF : (h + 1) * HALF]
+        w1_mx, w2_mx, wo_mx = mx_operand("w1", M), mx_operand("w2", M), mx_operand("wo", M)
+        x_mx, dy_mx = mx_operand("x", N), mx_operand("dy", N)
+        w1_bf, w2_bf, wo_bf = bf16_tile("w1", M), bf16_tile("w2", M), bf16_tile("wo", M)
+        x_bf = [bf16_tile("x" + str(h), HALF) for h in range(2)]
+        dy_bf = [bf16_tile("dy" + str(h), HALF) for h in range(2)]
 
         z1_bank = [ps.tile([P, N], F32, name="z1_bank" + str(g)) for g in range(G)]
-        z2_bank = [ps.tile([P, N], F32, name="z2_bank" + str(g)) for g in range(G)]
+        z2_c0_bank = [ps.tile([P, N], F32, name="z2_bank" + str(g)) for g in range(G)]
         q, t, lnq, p1, a, s, u, res = [per_group(n) for n in ("q", "t", "lnq", "p1", "a", "s", "u", "res")]
         sums = sb.tile([P, G], F32, name="sums")
-        nzs = sb.tile([P, G], F32, name="nzs")
-        nrz = sb.tile([P, G], F32, name="nrz")
+        zs = sb.tile([P, G], F32, name="zs")
+        recip = sb.tile([P, G], F32, name="recip")
         shift = sb.tile([P, G], F32, name="shift")
 
-        def columns(h):
-            return slice(h * HALF, (h + 1) * HALF)
-
-        def products(banks, w, moving, h):
+        def products(banks, weights, moving, h):
             for g in range(G):
-                product(banks[g], g, w, moving, h * HALF, (h + 1) * HALF)
+                rows = slice(ROWS * g, ROWS * (g + 1))
+                for c in range(h * HALF, (h + 1) * HALF, STEP):
+                    cols = slice(c, c + STEP)
+                    nc.tensor.matmul_mx(
+                        out=banks[g][:, cols],
+                        lhsT=weights[0][rows, :].bitcast(FP8X4),
+                        lhsT_scale=weights[1][rows, :],
+                        rhs=moving[0][rows, cols].bitcast(FP8X4),
+                        rhs_scale=moving[1][rows, cols],
+                        start=True,
+                        stop=True,
+                    )
 
         def sigmoids(h):
             for g in range(G):
@@ -115,47 +112,17 @@ def tile_rows_browshare_kernel(tc, x, w1, w2, re, wo, dy, old, out):
 
         def tanhs(h):
             for g in range(G):
-                nc.scalar.activation(out=t[g][:, columns(h)], in_=z2_bank[g][:, columns(h)], func=ACT.Tanh)
+                nc.scalar.activation(out=t[g][:, columns(h)], in_=z2_c0_bank[g][:, columns(h)], func=ACT.Tanh)
 
         def gradient(g, h):
-            nc.vector.tensor_tensor(out=a[g][:, columns(h)], in0=z2_bank[g][:, columns(h)], in1=t[g][:, columns(h)], op=ALU.mult)
-
-        interleave(x_b[0][:], x_raw[0])
-        interleave(w1_b[:], w1_raw)
-        quantize(*half(x_q, 0), x_b[0][:])
-        quantize(w1_q[0][:], w1_q[1][:], w1_b[:])
-        products(z1_bank, w1_q, x_q, 0)
-        sigmoids(0)
-        interleave(w2_b[:], w2_raw)
-        quantize(w2_q[0][:], w2_q[1][:], w2_b[:])
-        products(z2_bank, w2_q, x_q, 0)
-        tanhs(0)
-        interleave(x_b[1][:], x_raw[1])
-        quantize(*half(x_q, 1), x_b[1][:])
-        products(z2_bank, w2_q, x_q, 1)
-        tanhs(1)
-        products(z1_bank, w1_q, x_q, 1)
-        sigmoids(1)
-
-        interleave(wo_b[:], wo_raw)
-        quantize(wo_q[0][:], wo_q[1][:], wo_b[:])
-        interleave(dy_b[0][:], dy_raw[0])
-        quantize(*half(dy_q, 0), dy_b[0][:])
-        products(z2_bank, wo_q, dy_q, 0)
-        interleave(dy_b[1][:], dy_raw[1])
-        gradient(0, 0)
-        quantize(*half(dy_q, 1), dy_b[1][:])
-        for g in range(1, G):
-            gradient(g, 0)
-        products(z2_bank, wo_q, dy_q, 1)
-        for g in range(G):
-            gradient(g, 1)
+            cols = columns(h)
+            nc.vector.tensor_tensor(out=a[g][:, cols], in0=z2_c0_bank[g][:, cols], in1=t[g][:, cols], op=ALU.mult)
 
         def log(g):
             nc.scalar.activation(out=lnq[g][:], in_=q[g][:], func=ACT.Ln, bias=tiny[:])
 
-        def sigmoid(g):
-            nc.scalar.activation(out=s[g][:], in_=q[g][:], func=ACT.Copy, scale=-512.0, bias=512.0)
+        def scaled_sigmoid(g):
+            nc.scalar.activation(out=s[g][:], in_=q[g][:], func=ACT.Copy, scale=-SHARE, bias=SHARE)
 
         def softplus(g):
             nc.vector.scalar_tensor_tensor(
@@ -163,55 +130,98 @@ def tile_rows_browshare_kernel(tc, x, w1, w2, re, wo, dy, old, out):
                 op0=ALU.mult, op1=ALU.max, accum_out=sums[:, g : g + 1])
 
         def total(g):
-            nc.scalar.activation(out=nzs[:, g : g + 1], in_=sums[:, g : g + 1], func=ACT.Identity, bias=reserve[:, g : g + 1])
+            nc.scalar.activation(out=zs[:, g : g + 1], in_=sums[:, g : g + 1], func=ACT.Identity, bias=reserve[:, g : g + 1])
 
-        def invert(gs):
-            nc.vector.reciprocal(out=nrz[:, gs], in_=nzs[:, gs])
+        def invert(groups):
+            nc.vector.reciprocal(out=recip[:, groups], in_=zs[:, groups])
 
         def row_shift(g):
             nc.vector.scalar_tensor_tensor(
-                out=lnq[g][:], in0=a[g][:], scalar=nrz[:, g : g + 1], in1=p1[g][:],
+                out=lnq[g][:], in0=a[g][:], scalar=recip[:, g : g + 1], in1=p1[g][:],
                 op0=ALU.mult, op1=ALU.mult, accum_out=shift[:, g : g + 1])
 
-        def gate(g):
+        def row_products(g):
+            nc.gpsimd.tensor_tensor(out=lnq[g][:], in0=a[g][:], in1=p1[g][:], op=ALU.mult)
+
+        def row_sum(g):
+            nc.scalar.activation(
+                out=lnq[g][:], in_=lnq[g][:], func=ACT.Identity, scale=recip[:, g : g + 1],
+                accum_out=shift[:, g : g + 1])
+
+        def gate(g, cols):
             nc.vector.scalar_tensor_tensor(
-                out=u[g][:], in0=a[g][:], scalar=shift[:, g : g + 1], in1=s[g][:],
+                out=u[g][:, cols], in0=a[g][:, cols], scalar=shift[:, g : g + 1], in1=s[g][:, cols],
                 op0=ALU.subtract, op1=ALU.mult)
 
-        def finish(g, cols=slice(0, N), queue=nc.sync):
+        def finish(g, cols, queue):
             nc.vector.scalar_tensor_tensor(
-                out=res[g][:, cols], in0=u[g][:, cols], scalar=nrz[:, g : g + 1], in1=old_sb[:, g, cols],
+                out=res[g][:, cols], in0=u[g][:, cols], scalar=recip[:, g : g + 1], in1=old_sb[:, g, cols],
                 op0=ALU.mult, op1=ALU.add)
             queue.dma_start(out=out[g, :, cols], in_=res[g][:, cols])
 
-        log(0)
-        softplus(0)
-        log(1)
-        softplus(1)
-        log(2)
-        total(0)
-        softplus(2)
-        log(3)
-        total(1)
-        invert(slice(0, 1))
-        softplus(3)
-        sigmoid(0)
-        total(2)
-        total(3)
+        interleave(x_bf[0], x_raw[0])
+        interleave(w1_bf, w1_raw)
+        quantize(x_mx, columns(0), x_bf[0])
+        quantize(w1_mx, all_m, w1_bf)
+        products(z1_bank, w1_mx, x_mx, 0)
+        sigmoids(0)
+        interleave(w2_bf, w2_raw)
+        quantize(w2_mx, all_m, w2_bf)
+        products(z2_c0_bank, w2_mx, x_mx, 0)
+        tanhs(0)
+        interleave(x_bf[1], x_raw[1])
+        quantize(x_mx, columns(1), x_bf[1])
+        products(z2_c0_bank, w2_mx, x_mx, 1)
+        tanhs(1)
+        products(z1_bank, w1_mx, x_mx, 1)
+        sigmoids(1)
+
+        interleave(wo_bf, wo_raw)
+        quantize(wo_mx, all_m, wo_bf)
+        interleave(dy_bf[0], dy_raw[0])
+        quantize(dy_mx, columns(0), dy_bf[0])
+        products(z2_c0_bank, wo_mx, dy_mx, 0)
+        interleave(dy_bf[1], dy_raw[1])
+        gradient(0, 0)
+        quantize(dy_mx, columns(1), dy_bf[1])
         for g in range(1, G):
-            sigmoid(g)
+            gradient(g, 0)
+        products(z2_c0_bank, wo_mx, dy_mx, 1)
+        for g in range(G):
+            gradient(g, 1)
+
+        last = G - 1
+        all_n = slice(0, N)
+        log(last)
+        softplus(last)
+        row_products(last)
+        for g in range(last):
+            log(g)
+        softplus(0)
+        softplus(1)
+        total(0)
+        invert(slice(0, 1))
+        softplus(2)
+        total(1)
+        total(last)
+        scaled_sigmoid(0)
+        total(2)
         invert(slice(1, 2))
         row_shift(0)
-        invert(slice(2, 4))
+        invert(slice(2, G))
         row_shift(1)
-        gate(0)
+        scaled_sigmoid(1)
+        scaled_sigmoid(2)
+        row_sum(last)
+        scaled_sigmoid(last)
+        gate(0, all_n)
         row_shift(2)
-        finish(0)
-        gate(1)
-        row_shift(3)
-        finish(1)
-        gate(2)
-        gate(3)
-        finish(2)
-        finish(3, slice(0, HALF), nc.scalar)
-        finish(3, slice(HALF, N))
+        finish(0, all_n, nc.sync)
+        gate(1, all_n)
+        gate(2, all_n)
+        finish(1, all_n, nc.sync)
+        gate(last, columns(0))
+        finish(last - 1, all_n, nc.sync)
+        gate(last, columns(1))
+        finish(last, columns(0), nc.scalar)
+        finish(last, columns(1), nc.sync)

from contextlib import ExitStack

import concourse.mybir as mybir

G, D, M, N = 4, 128, 128, 512
P = 128
PACK = 4
ROWS = D // PACK
HALF = N // 2
RUN = 4
STEP = 128
SHARE = 512.0
TINY = 2.0 ** -63

F32 = mybir.dt.float32
BF16 = mybir.dt.bfloat16
U32 = mybir.dt.uint32
U8 = mybir.dt.uint8
FP8X4 = mybir.dt.float8_e4m3fn_x4
ACT = mybir.ActivationFunctionType
ALU = mybir.AluOpType

FLOPS = 3 * 2 * G * D * M * N


def tile_rows_browshare_kernel(tc, x, w1, w2, re, wo, dy, old, out):
    nc = tc.nc
    with ExitStack() as ctx:
        sb = ctx.enter_context(tc.tile_pool(name="sb", bufs=1))
        ps = ctx.enter_context(tc.psum_pool(name="ps", bufs=1))
        ctx.enter_context(tc.manual_schedule())

        def columns(h):
            return slice(h * HALF, (h + 1) * HALF)

        def load(name, src, cols):
            raw = sb.tile([P, PACK, cols.stop - cols.start], F32, name=name + "_raw", align_bytes=64)
            rows = src.rearrange("g (p j) c -> (g p) j c", j=PACK)
            nc.sync.dma_start(out=raw[:], in_=rows[:, :, cols])
            return raw

        def interleave(grouped, raw):
            nc.vector.tensor_copy(
                out=grouped[:].rearrange("p (c i j) -> p c j i", i=RUN, j=PACK),
                in_=raw[:].rearrange("p j (c i) -> p c j i", i=RUN),
            )

        def quantize(operand, cols, grouped):
            codes, scales = operand
            nc.vector.quantize_mx(out=codes[:, cols].bitcast(FP8X4), scales=scales[:, cols], in_=grouped[:])

        def mx_operand(name, width):
            codes = sb.tile([P, width], U32, name=name + "_codes", align_bytes=64)
            scales = sb.tile([P, width], U8, name=name + "_scales", align_bytes=64)
            return codes, scales

        def bf16_tile(name, width):
            grouped = sb.tile([P, PACK * width], BF16, name=name + "_bf16", align_bytes=64)
            return grouped

        def per_group(name):
            return [sb.tile([P, N], F32, name=name + str(g), align_bytes=64) for g in range(G)]

        all_m = slice(0, M)
        x_raw = [load("x0", x, columns(0))]
        w1_raw = load("w1", w1, all_m)
        w2_raw = load("w2", w2, all_m)
        x_raw.append(load("x1", x, columns(1)))
        wo_raw = load("wo", wo, all_m)
        dy_raw = [load("dy" + str(h), dy, columns(h)) for h in range(2)]
        reserve = sb.tile([P, G], F32, name="reserve")
        with nc.allow_non_contiguous_dma(reason="one reserve for each partition and group"):
            nc.sync.dma_start(out=reserve[:], in_=re.rearrange("g m o -> m (g o)"))
        old_sb = sb.tile([P, G, N], F32, name="old_sb")
        nc.sync.dma_start(out=old_sb[:], in_=old.rearrange("g m n -> m g n"))

        tiny = sb.tile([P, 1], F32, name="tiny")
        nc.vector.memset(tiny[:], TINY)

        w1_mx, w2_mx, wo_mx = mx_operand("w1", M), mx_operand("w2", M), mx_operand("wo", M)
        x_mx, dy_mx = mx_operand("x", N), mx_operand("dy", N)
        w1_bf, w2_bf, wo_bf = bf16_tile("w1", M), bf16_tile("w2", M), bf16_tile("wo", M)
        x_bf = [bf16_tile("x" + str(h), HALF) for h in range(2)]
        dy_bf = [bf16_tile("dy" + str(h), HALF) for h in range(2)]

        z1_bank = [ps.tile([P, N], F32, name="z1_bank" + str(g)) for g in range(G)]
        z2_c0_bank = [ps.tile([P, N], F32, name="z2_bank" + str(g)) for g in range(G)]
        q, t, lnq, p1, a, s, u, res = [per_group(n) for n in ("q", "t", "lnq", "p1", "a", "s", "u", "res")]
        sums = sb.tile([P, G], F32, name="sums")
        zs = sb.tile([P, G], F32, name="zs")
        recip = sb.tile([P, G], F32, name="recip")
        shift = sb.tile([P, G], F32, name="shift")

        def products(banks, weights, moving, h):
            for g in range(G):
                rows = slice(ROWS * g, ROWS * (g + 1))
                for c in range(h * HALF, (h + 1) * HALF, STEP):
                    cols = slice(c, c + STEP)
                    nc.tensor.matmul_mx(
                        out=banks[g][:, cols],
                        lhsT=weights[0][rows, :].bitcast(FP8X4),
                        lhsT_scale=weights[1][rows, :],
                        rhs=moving[0][rows, cols].bitcast(FP8X4),
                        rhs_scale=moving[1][rows, cols],
                        start=True,
                        stop=True,
                    )

        def sigmoids(h):
            for g in range(G):
                nc.scalar.activation(out=q[g][:, columns(h)], in_=z1_bank[g][:, columns(h)], func=ACT.Sigmoid, scale=-1.0)

        def tanhs(h):
            for g in range(G):
                nc.scalar.activation(out=t[g][:, columns(h)], in_=z2_c0_bank[g][:, columns(h)], func=ACT.Tanh)

        def gradient(g, h):
            cols = columns(h)
            nc.vector.tensor_tensor(out=a[g][:, cols], in0=z2_c0_bank[g][:, cols], in1=t[g][:, cols], op=ALU.mult)

        def log(g):
            nc.scalar.activation(out=lnq[g][:], in_=q[g][:], func=ACT.Ln, bias=tiny[:])

        def scaled_sigmoid(g):
            nc.scalar.activation(out=s[g][:], in_=q[g][:], func=ACT.Copy, scale=-SHARE, bias=SHARE)

        def softplus(g):
            nc.vector.scalar_tensor_tensor(
                out=p1[g][:], in0=lnq[g][:], scalar=-1.0, in1=z1_bank[g][:],
                op0=ALU.mult, op1=ALU.max, accum_out=sums[:, g : g + 1])

        def total(g):
            nc.scalar.activation(out=zs[:, g : g + 1], in_=sums[:, g : g + 1], func=ACT.Identity, bias=reserve[:, g : g + 1])

        def invert(groups):
            nc.vector.reciprocal(out=recip[:, groups], in_=zs[:, groups])

        def row_shift(g):
            nc.vector.scalar_tensor_tensor(
                out=lnq[g][:], in0=a[g][:], scalar=recip[:, g : g + 1], in1=p1[g][:],
                op0=ALU.mult, op1=ALU.mult, accum_out=shift[:, g : g + 1])

        def row_products(g):
            nc.gpsimd.tensor_tensor(out=lnq[g][:], in0=a[g][:], in1=p1[g][:], op=ALU.mult)

        def row_sum(g):
            nc.scalar.activation(
                out=lnq[g][:], in_=lnq[g][:], func=ACT.Identity, scale=recip[:, g : g + 1],
                accum_out=shift[:, g : g + 1])

        def gate(g, cols):
            nc.vector.scalar_tensor_tensor(
                out=u[g][:, cols], in0=a[g][:, cols], scalar=shift[:, g : g + 1], in1=s[g][:, cols],
                op0=ALU.subtract, op1=ALU.mult)

        def finish(g, cols, queue):
            nc.vector.scalar_tensor_tensor(
                out=res[g][:, cols], in0=u[g][:, cols], scalar=recip[:, g : g + 1], in1=old_sb[:, g, cols],
                op0=ALU.mult, op1=ALU.add)
            queue.dma_start(out=out[g, :, cols], in_=res[g][:, cols])

        interleave(x_bf[0], x_raw[0])
        interleave(w1_bf, w1_raw)
        quantize(x_mx, columns(0), x_bf[0])
        quantize(w1_mx, all_m, w1_bf)
        products(z1_bank, w1_mx, x_mx, 0)
        sigmoids(0)
        interleave(w2_bf, w2_raw)
        quantize(w2_mx, all_m, w2_bf)
        products(z2_c0_bank, w2_mx, x_mx, 0)
        tanhs(0)
        interleave(x_bf[1], x_raw[1])
        quantize(x_mx, columns(1), x_bf[1])
        products(z2_c0_bank, w2_mx, x_mx, 1)
        tanhs(1)
        products(z1_bank, w1_mx, x_mx, 1)
        sigmoids(1)

        interleave(wo_bf, wo_raw)
        quantize(wo_mx, all_m, wo_bf)
        interleave(dy_bf[0], dy_raw[0])
        quantize(dy_mx, columns(0), dy_bf[0])
        products(z2_c0_bank, wo_mx, dy_mx, 0)
        interleave(dy_bf[1], dy_raw[1])
        gradient(0, 0)
        quantize(dy_mx, columns(1), dy_bf[1])
        for g in range(1, G):
            gradient(g, 0)
        products(z2_c0_bank, wo_mx, dy_mx, 1)
        for g in range(G):
            gradient(g, 1)

        last = G - 1
        all_n = slice(0, N)
        log(last)
        softplus(last)
        row_products(last)
        for g in range(last):
            log(g)
        softplus(0)
        softplus(1)
        total(0)
        invert(slice(0, 1))
        softplus(2)
        total(1)
        total(last)
        scaled_sigmoid(0)
        total(2)
        invert(slice(1, 2))
        row_shift(0)
        invert(slice(2, G))
        row_shift(1)
        scaled_sigmoid(1)
        scaled_sigmoid(2)
        row_sum(last)
        scaled_sigmoid(last)
        gate(0, all_n)
        row_shift(2)
        finish(0, all_n, nc.sync)
        gate(1, all_n)
        gate(2, all_n)
        finish(1, all_n, nc.sync)
        gate(last, columns(0))
        finish(last - 1, all_n, nc.sync)
        gate(last, columns(1))
        finish(last, columns(0), nc.scalar)
        finish(last, columns(1), nc.sync)
